import numpy as np
import ml_dtypes


def mxq(x, axis, fmt="e4m3"):
    dtype, down = {"e4m3": (ml_dtypes.float8_e4m3fn, 7), "e5m2": (ml_dtypes.float8_e5m2, 14)}[fmt]
    v = np.moveaxis(np.asarray(x, np.float32).astype(ml_dtypes.bfloat16).astype(np.float64), axis, -1)
    blocks = v.reshape(v.shape[:-1] + (-1, 32))
    amax = np.abs(blocks).max(-1, keepdims=True)
    byte = np.maximum(np.where(amax > 0, np.frexp(amax)[1] - 1 + 127, 0) - down, 1)
    scale = np.exp2(byte - 127.0)
    codes = (blocks / scale).astype(np.float32).astype(dtype).astype(np.float64)
    return np.moveaxis((codes * scale).reshape(v.shape), -1, axis)


WIDE = False


def mx_kscale(k):
    if not WIDE:
        return np.ones(k)
    levels = np.array([30, -30])
    if k % 512:
        return np.exp2(np.random.permutation(np.resize(levels, k // 32))).repeat(32)
    a = np.empty((k // 512, 16))
    for p in range(k // 512):
        a[p, :8] = np.random.permutation(np.resize(levels, 8))
        for g in range(8):
            far = levels[np.abs(levels - a[p, g]) >= 10]
            a[p, g + 8] = far[np.random.randint(len(far))]
    return np.exp2(a.ravel()).repeat(32)


def f64(x):
    return np.asarray(x).astype(np.float64)


def striped(idx):
    return np.tile(np.asarray(idx).reshape(-1, 16).T, (8, 1)).astype(np.uint16)


def unstriped(offs):
    return offs[:16].T.reshape(-1).astype(np.int64)


E2M1 = np.array([0.0, 0.5, 1.0, 1.5, 2.0, 3.0, 4.0, 6.0, -0.0, -0.5, -1.0, -1.5, -2.0, -3.0, -4.0, -6.0])


def pack_weight(w, fmt):
    k, n = w.shape
    w = f64(np.asarray(w, np.float32).astype(ml_dtypes.bfloat16)).reshape(k // 32, 32, n)
    amax = np.abs(w).max(1)
    if fmt == "e4m3":
        byte = np.frexp(amax)[1] - 1 + 127 - 7
    else:
        mant, ex = np.frexp(amax / 6.0)
        byte = np.where(mant > 0.5, ex, ex - 1) + 127
    byte = np.clip(np.where(amax > 0, byte, 1), 1, 254)
    scaled = (w * np.exp2(127.0 - byte)[:, None, :]).reshape(k, n).astype(np.float32)
    by_word = np.ascontiguousarray(scaled.reshape(k // 512, 128, 4, n).transpose(0, 1, 3, 2))
    if fmt == "e4m3":
        words = by_word.astype(ml_dtypes.float8_e4m3fn).view(np.uint8)
    else:
        c = by_word.astype(ml_dtypes.float4_e2m1fn).view(np.uint8) & 0xF
        words = (c[..., 0::2] | (c[..., 1::2] << 4)).reshape(k // 512, 128, 2 * n)
    return np.ascontiguousarray(words), np.ascontiguousarray(byte.astype(np.uint8).reshape(k // 512, 16, n))


def unpack_weight(words, scales, fmt):
    g, _, n = scales.shape
    words = np.ascontiguousarray(words).reshape(g, 128, n, -1)
    if fmt == "e4m3":
        vals = words.view(ml_dtypes.float8_e4m3fn).astype(np.float64)
    else:
        nib = np.empty((g, 128, n, 4), np.uint8)
        nib[..., 0::2] = words & 0xF
        nib[..., 1::2] = words >> 4
        vals = E2M1[nib]
    vals = vals * np.repeat(np.exp2(scales.astype(np.float64) - 127.0), 8, axis=1)[..., None]
    return vals.transpose(0, 1, 3, 2).reshape(g * 512, n)


K, T, J, R, F, Z, N, C = 512, 512, 256, 512, 512, 1024, 256, 1024


def setup_inputs():
    n = np.random.standard_normal
    idx = np.random.permutation(T)[:J]
    idx2 = np.random.permutation(Z)[:J]
    idx3 = np.random.permutation(C)[:J]
    fk = mx_kscale(K)
    fr = mx_kscale(R)
    ff = mx_kscale(F)
    wp = pack_weight(n((K, R)) * 1 / np.sqrt(K) * fk[:, None] * fr, "e2m1")
    xop = pack_weight(n((F, Z)) / ff[:, None], "e2m1")
    w2p = pack_weight(n((F, R)) * 1 / np.sqrt(F) * ff[:, None] * fr, "e2m1")
    wbp = pack_weight(n((R, N)) * 1 / np.sqrt(R) / fr[:, None], "e4m3")
    return {
        "xf": (n((K, T))).astype(np.float32),
        "ow": (n((K, J)) * 0.7).astype(np.float32),
        "fk": (np.random.uniform(0.5, 2.0, (K, 1)) / fk[:, None]).astype(np.float32),
        "w_words": wp[0],
        "w_scales": wp[1],
        "xo_words": xop[0],
        "xo_scales": xop[1],
        "w2_words": w2p[0],
        "w2_scales": w2p[1],
        "wb_words": wbp[0],
        "wb_scales": wbp[1],
        "old": (1.0 * n((N, C))).astype(np.float32),
        "offs": striped(idx),
        "offs2": striped(idx2),
        "offs3": striped(idx3),
    }


def reference(xf, ow, fk, w_words, w_scales, xo_words, xo_scales, w2_words, w2_scales, wb_words, wb_scales, old, offs, offs2, offs3):
    idx = unstriped(offs)
    idx2 = unstriped(offs2)
    idx3 = unstriped(offs3)
    wu = unpack_weight(w_words, w_scales, "e2m1")
    xou = unpack_weight(xo_words, xo_scales, "e2m1")
    w2u = unpack_weight(w2_words, w2_scales, "e2m1")
    wbu = unpack_weight(wb_words, wb_scales, "e4m3")
    u = (f64(xf)[:, idx] - f64(ow)) * f64(fk)
    uq = mxq(u, 0, "e4m3")
    a = wu.T @ uq
    xoidx2g = xou[:, idx2]
    q = w2u.T @ xoidx2g
    hid = np.abs(a - q)
    hidq = mxq(hid, 0, "e5m2")
    p = wbu.T @ hidq
    pp = np.zeros((N, C))
    pp[:, idx3] = p
    y = pp + 0.5 * f64(old)
    return y

@@ -1,0 +1,184 @@
+from contextlib import ExitStack
+
+import concourse.mybir as mybir
+
+F32 = mybir.dt.float32
+BF16 = mybir.dt.bfloat16
+I32 = mybir.dt.int32
+U32 = mybir.dt.uint32
+U16 = mybir.dt.uint16
+U8 = mybir.dt.uint8
+E4M3 = mybir.dt.float8_e4m3fn_x4
+E5M2 = mybir.dt.float8_e5m2_x4
+E2M1 = mybir.dt.float4_e2m1fn_x4
+ALU = mybir.AluOpType
+ACT = mybir.ActivationFunctionType
+
+K, T, J, R, F, Z, N, C = 512, 512, 256, 512, 512, 1024, 256, 1024
+FLOPS = 2 * K * R * J + 2 * F * R * J + 2 * R * N * J
+
+P = 128
+PACK = 4
+HALF = 128
+HALVES = J // HALF
+LIST_COLS = HALF // 16
+STORE_COLS = 512
+
+
+def load_scale_rows(queue, plane, scales):
+    for q in range(4):
+        queue.dma_start(out=plane[32 * q : 32 * q + 4, :].bitcast(I32), in_=scales[0, 4 * q : 4 * q + 4, :].bitcast(I32))
+
+
+def deal_columns(nc, dealt, raw, run):
+    nc.vector.tensor_copy(
+        out=dealt[:].rearrange("p (t c i) -> p c t i", t=PACK, i=run),
+        in_=raw[:].rearrange("p (c i t) -> p c t i", t=PACK, i=run),
+    )
+
+
+def tile_list_two_offsetpicks_other_absgap_scattered_kernel(
+    tc, xf, ow, fk, w_words, w_scales, xo_words, xo_scales, w2_words, w2_scales, wb_words, wb_scales, old, offs, offs2, offs3, out
+):
+    nc = tc.nc
+    with ExitStack() as ctx:
+        sb = ctx.enter_context(tc.tile_pool(name="sb", bufs=1))
+        psum = ctx.enter_context(tc.psum_pool(name="psum", bufs=1))
+
+        idx1 = sb.tile([P, J // 16], U16, name="idx1")
+        idx2 = sb.tile([P, J // 16], U16, name="idx2")
+        idx3 = sb.tile([P, J // 16], U16, name="idx3")
+        xf_pair = [sb.tile([P, 2 * T], F32, name="xf_pair%d" % u) for u in range(2)]
+        ow_sb = sb.tile([P, PACK, J], F32, name="ow_sb")
+        fk_sb = sb.tile([P, PACK], F32, name="fk_sb")
+        old_sb = sb.tile([P, 2, C], F32, name="old_sb")
+        xo_w = sb.tile([P, Z], U16, name="xo_w")
+        xo_s = sb.tile([P, Z], U8, name="xo_s")
+        w_w = sb.tile([P, R], U16, name="w_w")
+        w_s = sb.tile([P, R], U8, name="w_s")
+        w2_w = sb.tile([P, R], U16, name="w2_w")
+        w2_s = sb.tile([P, R], U8, name="w2_s")
+        wb_w = sb.tile([P, N], U32, name="wb_w", align_bytes=64)
+        wb_s = sb.tile([P, N], U8, name="wb_s", align_bytes=64)
+        page = [sb.tile([P, C], F32, name="page%d" % a) for a in range(2)]
+
+        for plane in (xo_s, w2_s, w_s, wb_s):
+            nc.vector.memset(plane[:].bitcast(I32), 0)
+        for a in range(2):
+            nc.vector.memset(page[a][:], 0.0)
+
+        xf_rows = xf.rearrange("(p t) c -> p (t c)", t=PACK)
+        nc.sync.dma_start(idx2[:], offs2)
+        nc.sync.dma_start(out=xo_w[:].bitcast(I32), in_=xo_words[0].bitcast(I32))
+        nc.sync.dma_start(idx1[:], offs)
+        nc.sync.dma_start(out=xf_pair[0][:], in_=xf_rows[:, : 2 * T])
+        load_scale_rows(nc.sync, xo_s, xo_scales)
+        nc.sync.dma_start(out=xf_pair[1][:], in_=xf_rows[:, 2 * T :])
+        load_scale_rows(nc.sync, w2_s, w2_scales)
+        nc.sync.dma_start(out=w2_w[:].bitcast(I32), in_=w2_words[0].bitcast(I32))
+        nc.sync.dma_start(out=w_w[:].bitcast(I32), in_=w_words[0].bitcast(I32))
+        nc.sync.dma_start(out=fk_sb[:], in_=fk.rearrange("(p t) o -> p (t o)", t=PACK))
+        load_scale_rows(nc.sync, w_s, w_scales)
+        nc.sync.dma_start(out=ow_sb[:], in_=ow.rearrange("(p t) j -> p t j", t=PACK))
+        nc.sync.dma_start(out=wb_w[:].bitcast(I32), in_=wb_words[0].rearrange("p n t -> p (n t)").bitcast(I32))
+        load_scale_rows(nc.sync, wb_s, wb_scales)
+        nc.sync.dma_start(idx3[:], offs3)
+        nc.sync.dma_start(out=old_sb[:], in_=old.rearrange("(a p) c -> p a c", p=P))
+
+        xg_w = sb.tile([P, J], U16, name="xg_w", align_bytes=64)
+        xg_s = sb.tile([P, J], U8, name="xg_s", align_bytes=64)
+        nc.vector.tensor_copy(xg_w[:], xo_w[:].indirect(idx2[:]))
+        nc.vector.tensor_copy(xg_s[:], xo_s[:].indirect(idx2[:]))
+
+        picked = [sb.tile([P, PACK, HALF], F32, name="picked%d" % h) for h in range(HALVES)]
+        for u in range(2):
+            for h in range(HALVES):
+                for e in range(2):
+                    window = xf_pair[u][:, e * T : (e + 1) * T]
+                    slots = idx1[:, h * LIST_COLS : (h + 1) * LIST_COLS]
+                    nc.scalar.activation(picked[h][:, 2 * u + e, :], window.indirect(slots), ACT.Copy)
+
+        wd_w = sb.tile([P, R], U16, name="wd_w", align_bytes=64)
+        wd_s = sb.tile([P, R], U8, name="wd_s", align_bytes=64)
+        w2d_w = sb.tile([P, R], U16, name="w2d_w", align_bytes=64)
+        w2d_s = sb.tile([P, R], U8, name="w2d_s", align_bytes=64)
+        deal_columns(nc, w2d_s, w2_s, 16)
+        deal_columns(nc, w2d_w, w2_w, 8)
+        deal_columns(nc, wd_w, w_w, 8)
+        deal_columns(nc, wd_s, w_s, 16)
+
+        gap = [psum.tile([P, PACK, HALF], F32, name="gap%d" % h) for h in range(HALVES)]
+        for h in range(HALVES):
+            cols = slice(h * HALF, (h + 1) * HALF)
+            for t in range(PACK):
+                rows = slice(t * P, (t + 1) * P)
+                nc.tensor.matmul_mx(
+                    out=gap[h][:, t, :],
+                    lhsT=w2d_w[:, rows].bitcast(E2M1),
+                    lhsT_scale=w2d_s[:, rows],
+                    rhs=xg_w[:, cols].bitcast(E2M1),
+                    rhs_scale=xg_s[:, cols],
+                    start=(t == 0),
+                    stop=False,
+                )
+
+        fk_spread = fk_sb[:].unsqueeze(1).unsqueeze(3).to_broadcast([P, HALF // 4, PACK, 4])
+        for h in range(HALVES):
+            cols = slice(h * HALF, (h + 1) * HALF)
+            diff = sb.tile([P, PACK, HALF], F32, name="diff%d" % h)
+            nc.vector.tensor_tensor(diff[:], ow_sb[:, :, cols], picked[h][:], ALU.subtract)
+            u_bf = sb.tile([P, HALF * PACK], BF16, name="u_bf%d" % h, align_bytes=64)
+            nc.vector.tensor_tensor(
+                u_bf[:].rearrange("p (c i t) -> p c t i", t=PACK, i=4),
+                diff[:].rearrange("p t (c i) -> p c t i", i=4),
+                fk_spread,
+                ALU.mult,
+            )
+            uq_w = sb.tile([P, HALF], U32, name="uq_w%d" % h, align_bytes=64)
+            uq_s = sb.tile([P, HALF], U8, name="uq_s%d" % h, align_bytes=64)
+            nc.vector.quantize_mx(out=uq_w[:].bitcast(E4M3), scales=uq_s[:], in_=u_bf[:])
+            for t in range(PACK):
+                rows = slice(t * P, (t + 1) * P)
+                nc.tensor.matmul_mx(
+                    out=gap[h][:, t, :],
+                    lhsT=wd_w[:, rows].bitcast(E2M1),
+                    lhsT_scale=wd_s[:, rows],
+                    rhs=uq_w[:].bitcast(E4M3),
+                    rhs_scale=uq_s[:],
+                    start=False,
+                    stop=(t == PACK - 1),
+                )
+
+        for h in range(HALVES):
+            hid = sb.tile([P, HALF, PACK], BF16, name="hid%d" % h, align_bytes=64)
+            nc.scalar.activation(hid[:], gap[h][:].rearrange("p t j -> p j t"), ACT.Abs)
+            hq_w = sb.tile([P, HALF], U32, name="hq_w%d" % h, align_bytes=64)
+            hq_s = sb.tile([P, HALF], U8, name="hq_s%d" % h, align_bytes=64)
+            nc.vector.quantize_mx(out=hq_w[:].bitcast(E5M2), scales=hq_s[:], in_=hid[:].rearrange("p j t -> p (j t)"))
+            places = idx3[:, h * LIST_COLS : (h + 1) * LIST_COLS]
+            for a in range(2):
+                rows = slice(a * P, (a + 1) * P)
+                prod = psum.tile([P, HALF], F32, name="prod%d_%d" % (h, a))
+                nc.tensor.matmul_mx(
+                    out=prod[:],
+                    lhsT=wb_w[:, rows].bitcast(E4M3),
+                    lhsT_scale=wb_s[:, rows],
+                    rhs=hq_w[:].bitcast(E5M2),
+                    rhs_scale=hq_s[:],
+                    start=True,
+                    stop=True,
+                )
+                staged = sb.tile([P, HALF], F32, name="staged%d_%d" % (h, a))
+                if a == 0:
+                    nc.vector.tensor_copy(staged[:], prod[:])
+                    nc.vector.tensor_copy(page[a][:].indirect(places), staged[:])
+                else:
+                    nc.scalar.copy(staged[:], prod[:])
+                    nc.scalar.activation(page[a][:].indirect(places), staged[:], ACT.Copy)
+
+        for a in range(2):
+            for c0 in range(0, C, STORE_COLS):
+                cols = slice(c0, c0 + STORE_COLS)
+                res = sb.tile([P, STORE_COLS], F32, name="res%d_%d" % (a, c0))
+                nc.vector.scalar_tensor_tensor(res[:], old_sb[:, a, cols], 0.5, page[a][:, cols], ALU.mult, ALU.add)
+                nc.sync.dma_start(out=out[a * P : (a + 1) * P, cols], in_=res[:])

@@ -22,12 +22,19 @@ PACK = 4
 HALF = 128
 HALVES = J // HALF
 LIST_COLS = HALF // 16
-STORE_COLS = 512
+STORE_EDGES = ((0, 512, 1024), (0, 512, 768, 1024))
 
 
-def load_scale_rows(queue, plane, scales):
-    for q in range(4):
+def load_scale_rows(queue, plane, scales, quadrants=range(4)):
+    for q in quadrants:
         queue.dma_start(out=plane[32 * q : 32 * q + 4, :].bitcast(I32), in_=scales[0, 4 * q : 4 * q + 4, :].bitcast(I32))
+
+
+def fill_scale_rows(queue, plane, scales):
+    words = scales.shape[2] // 4
+    for q in range(4):
+        rows = scales[0, 4 * q : 4 * q + 4, :].bitcast(I32)
+        queue.dma_start(out=plane[32 * q : 32 * q + 32, :].bitcast(I32), in_=rows.unsqueeze(0).to_broadcast([8, 4, words]))
 
 
 def deal_columns(nc, dealt, raw, run):
@@ -55,57 +62,76 @@ def tile_list_two_offsetpicks_other_absgap_scattered_kernel(
         xo_w = sb.tile([P, Z], U16, name="xo_w")
         xo_s = sb.tile([P, Z], U8, name="xo_s")
         w_w = sb.tile([P, R], U16, name="w_w")
-        w_s = sb.tile([P, R], U8, name="w_s")
+        w_s = sb.tile([P, R], U8, name="w_s", tag="late", align_bytes=64)
         w2_w = sb.tile([P, R], U16, name="w2_w")
         w2_s = sb.tile([P, R], U8, name="w2_s")
         wb_w = sb.tile([P, N], U32, name="wb_w", align_bytes=64)
         wb_s = sb.tile([P, N], U8, name="wb_s", align_bytes=64)
         page = [sb.tile([P, C], F32, name="page%d" % a) for a in range(2)]
 
-        for plane in (xo_s, w2_s, w_s, wb_s):
+        for plane in (xo_s, w_s, wb_s):
             nc.vector.memset(plane[:].bitcast(I32), 0)
         for a in range(2):
             nc.vector.memset(page[a][:], 0.0)
 
         xf_rows = xf.rearrange("(p t) c -> p (t c)", t=PACK)
+        nc.gpsimd.dma_start(out=fk_sb[:], in_=fk.rearrange("(p t) o -> p (t o)", t=PACK))
         nc.sync.dma_start(idx2[:], offs2)
         nc.sync.dma_start(out=xo_w[:].bitcast(I32), in_=xo_words[0].bitcast(I32))
         nc.sync.dma_start(idx1[:], offs)
+        fill_scale_rows(nc.sync, w2_s, w2_scales)
         nc.sync.dma_start(out=xf_pair[0][:], in_=xf_rows[:, : 2 * T])
-        load_scale_rows(nc.sync, xo_s, xo_scales)
         nc.sync.dma_start(out=xf_pair[1][:], in_=xf_rows[:, 2 * T :])
-        load_scale_rows(nc.sync, w2_s, w2_scales)
+        load_scale_rows(nc.sync, xo_s, xo_scales)
         nc.sync.dma_start(out=w2_w[:].bitcast(I32), in_=w2_words[0].bitcast(I32))
-        nc.sync.dma_start(out=w_w[:].bitcast(I32), in_=w_words[0].bitcast(I32))
-        nc.sync.dma_start(out=fk_sb[:], in_=fk.rearrange("(p t) o -> p (t o)", t=PACK))
-        load_scale_rows(nc.sync, w_s, w_scales)
         nc.sync.dma_start(out=ow_sb[:], in_=ow.rearrange("(p t) j -> p t j", t=PACK))
+        nc.sync.dma_start(out=w_w[:].bitcast(I32), in_=w_words[0].bitcast(I32))
+        nc.sync.dma_start(idx3[:], offs3)
+        load_scale_rows(nc.sync, w_s, w_scales)
         nc.sync.dma_start(out=wb_w[:].bitcast(I32), in_=wb_words[0].rearrange("p n t -> p (n t)").bitcast(I32))
         load_scale_rows(nc.sync, wb_s, wb_scales)
-        nc.sync.dma_start(idx3[:], offs3)
         nc.sync.dma_start(out=old_sb[:], in_=old.rearrange("(a p) c -> p a c", p=P))
 
         xg_w = sb.tile([P, J], U16, name="xg_w", align_bytes=64)
         xg_s = sb.tile([P, J], U8, name="xg_s", align_bytes=64)
-        nc.vector.tensor_copy(xg_w[:], xo_w[:].indirect(idx2[:]))
-        nc.vector.tensor_copy(xg_s[:], xo_s[:].indirect(idx2[:]))
-
-        picked = [sb.tile([P, PACK, HALF], F32, name="picked%d" % h) for h in range(HALVES)]
-        for u in range(2):
-            for h in range(HALVES):
-                for e in range(2):
-                    window = xf_pair[u][:, e * T : (e + 1) * T]
-                    slots = idx1[:, h * LIST_COLS : (h + 1) * LIST_COLS]
-                    nc.scalar.activation(picked[h][:, 2 * u + e, :], window.indirect(slots), ACT.Copy)
-
         wd_w = sb.tile([P, R], U16, name="wd_w", align_bytes=64)
         wd_s = sb.tile([P, R], U8, name="wd_s", align_bytes=64)
         w2d_w = sb.tile([P, R], U16, name="w2d_w", align_bytes=64)
         w2d_s = sb.tile([P, R], U8, name="w2d_s", align_bytes=64)
+        nc.vector.tensor_copy(xg_w[:], xo_w[:].indirect(idx2[:]))
         deal_columns(nc, w2d_s, w2_s, 16)
+        nc.vector.tensor_copy(xg_s[:], xo_s[:].indirect(idx2[:]))
         deal_columns(nc, w2d_w, w2_w, 8)
+
+        picked = [sb.tile([P, PACK, HALF], F32, name="picked%d" % h) for h in range(HALVES)]
+        for u in range(2):
+            for h in range(HALVES):
+                slots = idx1[:, h * LIST_COLS : (h + 1) * LIST_COLS]
+                for e in range(2):
+                    window = xf_pair[u][:, e * T : (e + 1) * T]
+                    nc.scalar.activation(picked[h][:, 2 * u + e, :], window.indirect(slots), ACT.Copy)
+
+        fk_spread = fk_sb[:].unsqueeze(1).unsqueeze(3).to_broadcast([P, HALF // 4, PACK, 4])
+        uq_w = [sb.tile([P, HALF], U32, name="uq_w%d" % h, align_bytes=64) for h in range(HALVES)]
+        uq_s = [sb.tile([P, HALF], U8, name="uq_s%d" % h, align_bytes=64) for h in range(HALVES)]
+
+        def quantise_u(h):
+            cols = slice(h * HALF, (h + 1) * HALF)
+            diff = sb.tile([P, PACK, HALF], F32, name="diff%d" % h)
+            nc.vector.tensor_tensor(diff[:], ow_sb[:, :, cols], picked[h][:], ALU.subtract)
+            u_bf = sb.tile([P, HALF * PACK], BF16, name="u_bf%d" % h, tag=("early", "late")[h], align_bytes=64)
+            nc.vector.tensor_tensor(
+                u_bf[:].rearrange("p (c i t) -> p c t i", t=PACK, i=4),
+                diff[:].rearrange("p t (c i) -> p c t i", i=4),
+                fk_spread,
+                ALU.mult,
+            )
+            nc.vector.quantize_mx(out=uq_w[h][:].bitcast(E4M3), scales=uq_s[h][:], in_=u_bf[:])
+
+        quantise_u(0)
         deal_columns(nc, wd_w, w_w, 8)
         deal_columns(nc, wd_s, w_s, 16)
+        quantise_u(1)
 
         gap = [psum.tile([P, PACK, HALF], F32, name="gap%d" % h) for h in range(HALVES)]
         for h in range(HALVES):
@@ -121,30 +147,14 @@ def tile_list_two_offsetpicks_other_absgap_scattered_kernel(
                     start=(t == 0),
                     stop=False,
                 )
-
-        fk_spread = fk_sb[:].unsqueeze(1).unsqueeze(3).to_broadcast([P, HALF // 4, PACK, 4])
-        for h in range(HALVES):
-            cols = slice(h * HALF, (h + 1) * HALF)
-            diff = sb.tile([P, PACK, HALF], F32, name="diff%d" % h)
-            nc.vector.tensor_tensor(diff[:], ow_sb[:, :, cols], picked[h][:], ALU.subtract)
-            u_bf = sb.tile([P, HALF * PACK], BF16, name="u_bf%d" % h, align_bytes=64)
-            nc.vector.tensor_tensor(
-                u_bf[:].rearrange("p (c i t) -> p c t i", t=PACK, i=4),
-                diff[:].rearrange("p t (c i) -> p c t i", i=4),
-                fk_spread,
-                ALU.mult,
-            )
-            uq_w = sb.tile([P, HALF], U32, name="uq_w%d" % h, align_bytes=64)
-            uq_s = sb.tile([P, HALF], U8, name="uq_s%d" % h, align_bytes=64)
-            nc.vector.quantize_mx(out=uq_w[:].bitcast(E4M3), scales=uq_s[:], in_=u_bf[:])
             for t in range(PACK):
                 rows = slice(t * P, (t + 1) * P)
                 nc.tensor.matmul_mx(
                     out=gap[h][:, t, :],
                     lhsT=wd_w[:, rows].bitcast(E2M1),
                     lhsT_scale=wd_s[:, rows],
-                    rhs=uq_w[:].bitcast(E4M3),
-                    rhs_scale=uq_s[:],
+                    rhs=uq_w[h][:].bitcast(E4M3),
+                    rhs_scale=uq_s[h][:],
                     start=False,
                     stop=(t == PACK - 1),
                 )
@@ -177,8 +187,8 @@ def tile_list_two_offsetpicks_other_absgap_scattered_kernel(
                     nc.scalar.activation(page[a][:].indirect(places), staged[:], ACT.Copy)
 
         for a in range(2):
-            for c0 in range(0, C, STORE_COLS):
-                cols = slice(c0, c0 + STORE_COLS)
-                res = sb.tile([P, STORE_COLS], F32, name="res%d_%d" % (a, c0))
+            for c0, c1 in zip(STORE_EDGES[a], STORE_EDGES[a][1:]):
+                cols = slice(c0, c1)
+                res = sb.tile([P, c1 - c0], F32, name="res%d_%d" % (a, c0))
                 nc.vector.scalar_tensor_tensor(res[:], old_sb[:, a, cols], 0.5, page[a][:, cols], ALU.mult, ALU.add)
                 nc.sync.dma_start(out=out[a * P : (a + 1) * P, cols], in_=res[:])

@@ -22,7 +22,7 @@ PACK = 4
 HALF = 128
 HALVES = J // HALF
 LIST_COLS = HALF // 16
-STORE_EDGES = ((0, 512, 1024), (0, 512, 768, 1024))
+STORE_EDGES = ((0, 256, 640, 1024), (0, 512, 768, 1024))
 
 
 def load_scale_rows(queue, plane, scales, quadrants=range(4)):
@@ -56,7 +56,7 @@ def tile_list_two_offsetpicks_other_absgap_scattered_kernel(
         idx2 = sb.tile([P, J // 16], U16, name="idx2")
         idx3 = sb.tile([P, J // 16], U16, name="idx3")
         xf_pair = [sb.tile([P, 2 * T], F32, name="xf_pair%d" % u) for u in range(2)]
-        ow_sb = sb.tile([P, PACK, J], F32, name="ow_sb")
+        ow_pair = [sb.tile([P, 2, J], F32, name="ow_pair%d" % u) for u in range(2)]
         fk_sb = sb.tile([P, PACK], F32, name="fk_sb")
         old_sb = sb.tile([P, 2, C], F32, name="old_sb")
         xo_w = sb.tile([P, Z], U16, name="xo_w")
@@ -71,11 +71,14 @@ def tile_list_two_offsetpicks_other_absgap_scattered_kernel(
 
         for plane in (xo_s, w_s, wb_s):
             nc.vector.memset(plane[:].bitcast(I32), 0)
+        warm = sb.tile([P, 2], F32, name="warm")
+        nc.vector.memset(warm[:, 0:1], 0.0)
+        nc.scalar.activation(warm[:, 1:2], warm[:, 0:1], ACT.Abs)
         for a in range(2):
             nc.vector.memset(page[a][:], 0.0)
 
+        ow_rows = ow.rearrange("(p t) j -> p t j", t=PACK)
         xf_rows = xf.rearrange("(p t) c -> p (t c)", t=PACK)
-        nc.gpsimd.dma_start(out=fk_sb[:], in_=fk.rearrange("(p t) o -> p (t o)", t=PACK))
         nc.sync.dma_start(idx2[:], offs2)
         nc.sync.dma_start(out=xo_w[:].bitcast(I32), in_=xo_words[0].bitcast(I32))
         nc.sync.dma_start(idx1[:], offs)
@@ -84,12 +87,14 @@ def tile_list_two_offsetpicks_other_absgap_scattered_kernel(
         nc.sync.dma_start(out=xf_pair[1][:], in_=xf_rows[:, 2 * T :])
         load_scale_rows(nc.sync, xo_s, xo_scales)
         nc.sync.dma_start(out=w2_w[:].bitcast(I32), in_=w2_words[0].bitcast(I32))
-        nc.sync.dma_start(out=ow_sb[:], in_=ow.rearrange("(p t) j -> p t j", t=PACK))
+        nc.sync.dma_start(out=ow_pair[0][:], in_=ow_rows[:, 0:2, :])
+        nc.sync.dma_start(out=ow_pair[1][:], in_=ow_rows[:, 2:4, :])
         nc.sync.dma_start(out=w_w[:].bitcast(I32), in_=w_words[0].bitcast(I32))
-        nc.sync.dma_start(idx3[:], offs3)
+        nc.sync.dma_start(out=fk_sb[:], in_=fk.rearrange("(p t) o -> p (t o)", t=PACK))
         load_scale_rows(nc.sync, w_s, w_scales)
         nc.sync.dma_start(out=wb_w[:].bitcast(I32), in_=wb_words[0].rearrange("p n t -> p (n t)").bitcast(I32))
         load_scale_rows(nc.sync, wb_s, wb_scales)
+        nc.sync.dma_start(idx3[:], offs3)
         nc.sync.dma_start(out=old_sb[:], in_=old.rearrange("(a p) c -> p a c", p=P))
 
         xg_w = sb.tile([P, J], U16, name="xg_w", align_bytes=64)
@@ -113,25 +118,33 @@ def tile_list_two_offsetpicks_other_absgap_scattered_kernel(
 
         fk_spread = fk_sb[:].unsqueeze(1).unsqueeze(3).to_broadcast([P, HALF // 4, PACK, 4])
         uq_w = [sb.tile([P, HALF], U32, name="uq_w%d" % h, align_bytes=64) for h in range(HALVES)]
-        uq_s = [sb.tile([P, HALF], U8, name="uq_s%d" % h, align_bytes=64) for h in range(HALVES)]
-
-        def quantise_u(h):
-            cols = slice(h * HALF, (h + 1) * HALF)
-            diff = sb.tile([P, PACK, HALF], F32, name="diff%d" % h)
-            nc.vector.tensor_tensor(diff[:], ow_sb[:, :, cols], picked[h][:], ALU.subtract)
-            u_bf = sb.tile([P, HALF * PACK], BF16, name="u_bf%d" % h, tag=("early", "late")[h], align_bytes=64)
-            nc.vector.tensor_tensor(
-                u_bf[:].rearrange("p (c i t) -> p c t i", t=PACK, i=4),
-                diff[:].rearrange("p t (c i) -> p c t i", i=4),
-                fk_spread,
-                ALU.mult,
-            )
-            nc.vector.quantize_mx(out=uq_w[h][:].bitcast(E4M3), scales=uq_s[h][:], in_=u_bf[:])
-
-        quantise_u(0)
+        diff = [sb.tile([P, PACK, HALF], F32, name="diff%d" % h) for h in range(HALVES)]
+        u_bf = [sb.tile([P, HALF * PACK], BF16, name="u_bf%d" % h, align_bytes=64) for h in range(HALVES)]
+        for u in range(2):
+            planes = slice(2 * u, 2 * u + 2)
+            for h in range(HALVES):
+                centres = ow_pair[u][:, :, h * HALF : (h + 1) * HALF]
+                nc.vector.tensor_tensor(diff[h][:, planes, :], centres, picked[h][:, planes, :], ALU.subtract)
+        nc.vector.tensor_tensor(
+            u_bf[0][:].rearrange("p (c i t) -> p c t i", t=PACK, i=4),
+            diff[0][:].rearrange("p t (c i) -> p c t i", i=4),
+            fk_spread,
+            ALU.mult,
+        )
+        u_rows = sb.tile([P, PACK, HALF], BF16, name="u_rows")
+        for t in range(PACK):
+            nc.scalar.activation(u_rows[:, t, :], diff[1][:, t, :], ACT.Copy, scale=fk_sb[:, t : t + 1])
+        nc.scalar.copy(
+            u_bf[1][:].rearrange("p (c i t) -> p c t i", t=PACK, i=4),
+            u_rows[:].rearrange("p t (c i) -> p c t i", i=4),
+        )
         deal_columns(nc, wd_w, w_w, 8)
+        uq_s0 = sb.tile([P, HALF], U8, name="uq_s0", align_bytes=64)
+        nc.vector.quantize_mx(out=uq_w[0][:].bitcast(E4M3), scales=uq_s0[:], in_=u_bf[0][:])
         deal_columns(nc, wd_s, w_s, 16)
-        quantise_u(1)
+        uq_s1 = sb.tile([P, HALF], U8, name="uq_s1", tag="late", align_bytes=64)
+        nc.vector.quantize_mx(out=uq_w[1][:].bitcast(E4M3), scales=uq_s1[:], in_=u_bf[1][:])
+        uq_s = [uq_s0, uq_s1]
 
         gap = [psum.tile([P, PACK, HALF], F32, name="gap%d" % h) for h in range(HALVES)]
         for h in range(HALVES):
@@ -159,18 +172,18 @@ def tile_list_two_offsetpicks_other_absgap_scattered_kernel(
                     stop=(t == PACK - 1),
                 )
 
+        staged_hi = sb.tile([P, J], F32, name="staged_hi")
         for h in range(HALVES):
             hid = sb.tile([P, HALF, PACK], BF16, name="hid%d" % h, align_bytes=64)
             nc.scalar.activation(hid[:], gap[h][:].rearrange("p t j -> p j t"), ACT.Abs)
             hq_w = sb.tile([P, HALF], U32, name="hq_w%d" % h, align_bytes=64)
             hq_s = sb.tile([P, HALF], U8, name="hq_s%d" % h, align_bytes=64)
             nc.vector.quantize_mx(out=hq_w[:].bitcast(E5M2), scales=hq_s[:], in_=hid[:].rearrange("p j t -> p (j t)"))
-            places = idx3[:, h * LIST_COLS : (h + 1) * LIST_COLS]
+            prod = psum.tile([P, 2, HALF], F32, name="prod%d" % h)
             for a in range(2):
                 rows = slice(a * P, (a + 1) * P)
-                prod = psum.tile([P, HALF], F32, name="prod%d_%d" % (h, a))
                 nc.tensor.matmul_mx(
-                    out=prod[:],
+                    out=prod[:, a, :],
                     lhsT=wb_w[:, rows].bitcast(E4M3),
                     lhsT_scale=wb_s[:, rows],
                     rhs=hq_w[:].bitcast(E5M2),
@@ -178,13 +191,12 @@ def tile_list_two_offsetpicks_other_absgap_scattered_kernel(
                     start=True,
                     stop=True,
                 )
-                staged = sb.tile([P, HALF], F32, name="staged%d_%d" % (h, a))
-                if a == 0:
-                    nc.vector.tensor_copy(staged[:], prod[:])
-                    nc.vector.tensor_copy(page[a][:].indirect(places), staged[:])
-                else:
-                    nc.scalar.copy(staged[:], prod[:])
-                    nc.scalar.activation(page[a][:].indirect(places), staged[:], ACT.Copy)
+            staged = sb.tile([P, HALF], F32, name="staged%d" % h)
+            nc.scalar.copy(staged[:], prod[:, 0, :])
+            nc.scalar.copy(staged_hi[:, h * HALF : (h + 1) * HALF], prod[:, 1, :])
+            places = idx3[:, h * LIST_COLS : (h + 1) * LIST_COLS]
+            nc.vector.tensor_copy(page[0][:].indirect(places), staged[:])
+        nc.scalar.activation(page[1][:].indirect(idx3[:]), staged_hi[:], ACT.Copy)
 
         for a in range(2):
             for c0, c1 in zip(STORE_EDGES[a], STORE_EDGES[a][1:]):

from contextlib import ExitStack

import concourse.mybir as mybir

F32 = mybir.dt.float32
BF16 = mybir.dt.bfloat16
I32 = mybir.dt.int32
U32 = mybir.dt.uint32
U16 = mybir.dt.uint16
U8 = mybir.dt.uint8
E4M3 = mybir.dt.float8_e4m3fn_x4
E5M2 = mybir.dt.float8_e5m2_x4
E2M1 = mybir.dt.float4_e2m1fn_x4
ALU = mybir.AluOpType
ACT = mybir.ActivationFunctionType

K, T, J, R, F, Z, N, C = 512, 512, 256, 512, 512, 1024, 256, 1024
FLOPS = 2 * K * R * J + 2 * F * R * J + 2 * R * N * J

P = 128
PACK = 4
HALF = 128
HALVES = J // HALF
LIST_COLS = HALF // 16
STORE_EDGES = ((0, 256, 640, 1024), (0, 512, 768, 1024))


def load_scale_rows(queue, plane, scales, quadrants=range(4)):
    for q in quadrants:
        queue.dma_start(out=plane[32 * q : 32 * q + 4, :].bitcast(I32), in_=scales[0, 4 * q : 4 * q + 4, :].bitcast(I32))


def fill_scale_rows(queue, plane, scales):
    words = scales.shape[2] // 4
    for q in range(4):
        rows = scales[0, 4 * q : 4 * q + 4, :].bitcast(I32)
        queue.dma_start(out=plane[32 * q : 32 * q + 32, :].bitcast(I32), in_=rows.unsqueeze(0).to_broadcast([8, 4, words]))


def deal_columns(nc, dealt, raw, run):
    nc.vector.tensor_copy(
        out=dealt[:].rearrange("p (t c i) -> p c t i", t=PACK, i=run),
        in_=raw[:].rearrange("p (c i t) -> p c t i", t=PACK, i=run),
    )


def tile_list_two_offsetpicks_other_absgap_scattered_kernel(
    tc, xf, ow, fk, w_words, w_scales, xo_words, xo_scales, w2_words, w2_scales, wb_words, wb_scales, old, offs, offs2, offs3, out
):
    nc = tc.nc
    with ExitStack() as ctx:
        sb = ctx.enter_context(tc.tile_pool(name="sb", bufs=1))
        psum = ctx.enter_context(tc.psum_pool(name="psum", bufs=1))

        idx1 = sb.tile([P, J // 16], U16, name="idx1")
        idx2 = sb.tile([P, J // 16], U16, name="idx2")
        idx3 = sb.tile([P, J // 16], U16, name="idx3")
        xf_pair = [sb.tile([P, 2 * T], F32, name="xf_pair%d" % u) for u in range(2)]
        ow_pair = [sb.tile([P, 2, J], F32, name="ow_pair%d" % u) for u in range(2)]
        fk_sb = sb.tile([P, PACK], F32, name="fk_sb")
        old_sb = sb.tile([P, 2, C], F32, name="old_sb")
        xo_w = sb.tile([P, Z], U16, name="xo_w")
        xo_s = sb.tile([P, Z], U8, name="xo_s")
        w_w = sb.tile([P, R], U16, name="w_w")
        w_s = sb.tile([P, R], U8, name="w_s", tag="late", align_bytes=64)
        w2_w = sb.tile([P, R], U16, name="w2_w")
        w2_s = sb.tile([P, R], U8, name="w2_s")
        wb_w = sb.tile([P, N], U32, name="wb_w", align_bytes=64)
        wb_s = sb.tile([P, N], U8, name="wb_s", align_bytes=64)
        page = [sb.tile([P, C], F32, name="page%d" % a) for a in range(2)]

        for plane in (xo_s, w_s, wb_s):
            nc.vector.memset(plane[:].bitcast(I32), 0)
        warm = sb.tile([P, 2], F32, name="warm")
        nc.vector.memset(warm[:, 0:1], 0.0)
        nc.scalar.activation(warm[:, 1:2], warm[:, 0:1], ACT.Abs)
        for a in range(2):
            nc.vector.memset(page[a][:], 0.0)

        ow_rows = ow.rearrange("(p t) j -> p t j", t=PACK)
        xf_rows = xf.rearrange("(p t) c -> p (t c)", t=PACK)
        nc.sync.dma_start(idx2[:], offs2)
        nc.sync.dma_start(out=xo_w[:].bitcast(I32), in_=xo_words[0].bitcast(I32))
        nc.sync.dma_start(idx1[:], offs)
        fill_scale_rows(nc.sync, w2_s, w2_scales)
        nc.sync.dma_start(out=xf_pair[0][:], in_=xf_rows[:, : 2 * T])
        nc.sync.dma_start(out=xf_pair[1][:], in_=xf_rows[:, 2 * T :])
        load_scale_rows(nc.sync, xo_s, xo_scales)
        nc.sync.dma_start(out=w2_w[:].bitcast(I32), in_=w2_words[0].bitcast(I32))
        nc.sync.dma_start(out=ow_pair[0][:], in_=ow_rows[:, 0:2, :])
        nc.sync.dma_start(out=ow_pair[1][:], in_=ow_rows[:, 2:4, :])
        nc.sync.dma_start(out=w_w[:].bitcast(I32), in_=w_words[0].bitcast(I32))
        nc.sync.dma_start(out=fk_sb[:], in_=fk.rearrange("(p t) o -> p (t o)", t=PACK))
        load_scale_rows(nc.sync, w_s, w_scales)
        nc.sync.dma_start(out=wb_w[:].bitcast(I32), in_=wb_words[0].rearrange("p n t -> p (n t)").bitcast(I32))
        load_scale_rows(nc.sync, wb_s, wb_scales)
        nc.sync.dma_start(idx3[:], offs3)
        nc.sync.dma_start(out=old_sb[:], in_=old.rearrange("(a p) c -> p a c", p=P))

        xg_w = sb.tile([P, J], U16, name="xg_w", align_bytes=64)
        xg_s = sb.tile([P, J], U8, name="xg_s", align_bytes=64)
        wd_w = sb.tile([P, R], U16, name="wd_w", align_bytes=64)
        wd_s = sb.tile([P, R], U8, name="wd_s", align_bytes=64)
        w2d_w = sb.tile([P, R], U16, name="w2d_w", align_bytes=64)
        w2d_s = sb.tile([P, R], U8, name="w2d_s", align_bytes=64)
        nc.vector.tensor_copy(xg_w[:], xo_w[:].indirect(idx2[:]))
        deal_columns(nc, w2d_s, w2_s, 16)
        nc.vector.tensor_copy(xg_s[:], xo_s[:].indirect(idx2[:]))
        deal_columns(nc, w2d_w, w2_w, 8)

        picked = [sb.tile([P, PACK, HALF], F32, name="picked%d" % h) for h in range(HALVES)]
        for u in range(2):
            for h in range(HALVES):
                slots = idx1[:, h * LIST_COLS : (h + 1) * LIST_COLS]
                for e in range(2):
                    window = xf_pair[u][:, e * T : (e + 1) * T]
                    nc.scalar.activation(picked[h][:, 2 * u + e, :], window.indirect(slots), ACT.Copy)

        fk_spread = fk_sb[:].unsqueeze(1).unsqueeze(3).to_broadcast([P, HALF // 4, PACK, 4])
        uq_w = [sb.tile([P, HALF], U32, name="uq_w%d" % h, align_bytes=64) for h in range(HALVES)]
        diff = [sb.tile([P, PACK, HALF], F32, name="diff%d" % h) for h in range(HALVES)]
        u_bf = [sb.tile([P, HALF * PACK], BF16, name="u_bf%d" % h, align_bytes=64) for h in range(HALVES)]
        for u in range(2):
            planes = slice(2 * u, 2 * u + 2)
            for h in range(HALVES):
                centres = ow_pair[u][:, :, h * HALF : (h + 1) * HALF]
                nc.vector.tensor_tensor(diff[h][:, planes, :], centres, picked[h][:, planes, :], ALU.subtract)
        nc.vector.tensor_tensor(
            u_bf[0][:].rearrange("p (c i t) -> p c t i", t=PACK, i=4),
            diff[0][:].rearrange("p t (c i) -> p c t i", i=4),
            fk_spread,
            ALU.mult,
        )
        u_rows = sb.tile([P, PACK, HALF], BF16, name="u_rows")
        for t in range(PACK):
            nc.scalar.activation(u_rows[:, t, :], diff[1][:, t, :], ACT.Copy, scale=fk_sb[:, t : t + 1])
        nc.scalar.copy(
            u_bf[1][:].rearrange("p (c i t) -> p c t i", t=PACK, i=4),
            u_rows[:].rearrange("p t (c i) -> p c t i", i=4),
        )
        deal_columns(nc, wd_w, w_w, 8)
        uq_s0 = sb.tile([P, HALF], U8, name="uq_s0", align_bytes=64)
        nc.vector.quantize_mx(out=uq_w[0][:].bitcast(E4M3), scales=uq_s0[:], in_=u_bf[0][:])
        deal_columns(nc, wd_s, w_s, 16)
        uq_s1 = sb.tile([P, HALF], U8, name="uq_s1", tag="late", align_bytes=64)
        nc.vector.quantize_mx(out=uq_w[1][:].bitcast(E4M3), scales=uq_s1[:], in_=u_bf[1][:])
        uq_s = [uq_s0, uq_s1]

        gap = [psum.tile([P, PACK, HALF], F32, name="gap%d" % h) for h in range(HALVES)]
        for h in range(HALVES):
            cols = slice(h * HALF, (h + 1) * HALF)
            for t in range(PACK):
                rows = slice(t * P, (t + 1) * P)
                nc.tensor.matmul_mx(
                    out=gap[h][:, t, :],
                    lhsT=w2d_w[:, rows].bitcast(E2M1),
                    lhsT_scale=w2d_s[:, rows],
                    rhs=xg_w[:, cols].bitcast(E2M1),
                    rhs_scale=xg_s[:, cols],
                    start=(t == 0),
                    stop=False,
                )
            for t in range(PACK):
                rows = slice(t * P, (t + 1) * P)
                nc.tensor.matmul_mx(
                    out=gap[h][:, t, :],
                    lhsT=wd_w[:, rows].bitcast(E2M1),
                    lhsT_scale=wd_s[:, rows],
                    rhs=uq_w[h][:].bitcast(E4M3),
                    rhs_scale=uq_s[h][:],
                    start=False,
                    stop=(t == PACK - 1),
                )

        staged_hi = sb.tile([P, J], F32, name="staged_hi")
        for h in range(HALVES):
            hid = sb.tile([P, HALF, PACK], BF16, name="hid%d" % h, align_bytes=64)
            nc.scalar.activation(hid[:], gap[h][:].rearrange("p t j -> p j t"), ACT.Abs)
            hq_w = sb.tile([P, HALF], U32, name="hq_w%d" % h, align_bytes=64)
            hq_s = sb.tile([P, HALF], U8, name="hq_s%d" % h, align_bytes=64)
            nc.vector.quantize_mx(out=hq_w[:].bitcast(E5M2), scales=hq_s[:], in_=hid[:].rearrange("p j t -> p (j t)"))
            prod = psum.tile([P, 2, HALF], F32, name="prod%d" % h)
            for a in range(2):
                rows = slice(a * P, (a + 1) * P)
                nc.tensor.matmul_mx(
                    out=prod[:, a, :],
                    lhsT=wb_w[:, rows].bitcast(E4M3),
                    lhsT_scale=wb_s[:, rows],
                    rhs=hq_w[:].bitcast(E5M2),
                    rhs_scale=hq_s[:],
                    start=True,
                    stop=True,
                )
            staged = sb.tile([P, HALF], F32, name="staged%d" % h)
            nc.scalar.copy(staged[:], prod[:, 0, :])
            nc.scalar.copy(staged_hi[:, h * HALF : (h + 1) * HALF], prod[:, 1, :])
            places = idx3[:, h * LIST_COLS : (h + 1) * LIST_COLS]
            nc.vector.tensor_copy(page[0][:].indirect(places), staged[:])
        nc.scalar.activation(page[1][:].indirect(idx3[:]), staged_hi[:], ACT.Copy)

        for a in range(2):
            for c0, c1 in zip(STORE_EDGES[a], STORE_EDGES[a][1:]):
                cols = slice(c0, c1)
                res = sb.tile([P, c1 - c0], F32, name="res%d_%d" % (a, c0))
                nc.vector.scalar_tensor_tensor(res[:], old_sb[:, a, cols], 0.5, page[a][:, cols], ALU.mult, ALU.add)
                nc.sync.dma_start(out=out[a * P : (a + 1) * P, cols], in_=res[:])
